import numpy as np
import ml_dtypes

BF16 = ml_dtypes.bfloat16


def bf(x):
    return np.asarray(x, np.float32).astype(BF16)


def f32(x):
    return np.asarray(x, np.float32)


def f64(x):
    return np.asarray(x).astype(np.float64)


def striped(idx):
    return np.tile(idx.reshape(-1, 16).T, (8, 1))


def rows(idx, k):
    return np.tile(idx, (k, 1))


def look(tab, idx):
    return np.take_along_axis(f64(tab), rows(idx, len(tab)), axis=1)


K, S, V, N = 256, 2048, 1536, 1536


def setup_inputs():
    return {"tab": f32(np.random.standard_normal((2, K, S))), "offs": striped(np.random.permutation(S)[:N])}


def reference(tab, offs):
    idx = offs[:16].T.reshape(-1)
    x = (look(tab[0], idx) - 0.125) * 1.5 / (1.0 + np.exp(-look(tab[1], idx)))
    return x

@@ -1,0 +1,58 @@
+import concourse.mybir as mybir
+
+F32 = mybir.dt.float32
+U16 = mybir.dt.uint16
+ALU = mybir.AluOpType
+SIGMOID = mybir.ActivationFunctionType.Sigmoid
+
+P = 128
+STRIPE = 16
+PIECE = 512
+
+SHIFT = 0.125
+SCALE = 1.5
+
+
+def tile_lookup_gnorm_out_kernel(tc, tab, offs, out):
+    nc = tc.nc
+    tables, rows, places = tab.shape
+    assert tables == 2
+    entries = out.shape[1]
+    blocks = rows // P
+    pieces = entries // PIECE
+
+    with (
+        tc.tile_pool(name="held", bufs=1) as held,
+        tc.tile_pool(name="work", bufs=1) as work,
+    ):
+        offsets = held.tile([P, entries // STRIPE], U16, name="offsets")
+        nc.sync.dma_start(offsets[:], offs)
+
+        values = []
+        gates = []
+        for b in range(blocks):
+            block_rows = slice(b * P, (b + 1) * P)
+            value_window = held.tile([P, places], F32, name=f"value_window{b}")
+            nc.sync.dma_start(value_window[:], tab[0, block_rows, :])
+            gate_window = held.tile([P, places], F32, name=f"gate_window{b}")
+            nc.sync.dma_start(gate_window[:], tab[1, block_rows, :])
+            values.append(value_window)
+            gates.append(gate_window)
+
+        for b in range(blocks):
+            block_rows = slice(b * P, (b + 1) * P)
+            normed = []
+            for k in range(pieces):
+                listed = offsets[:, k * PIECE // STRIPE : (k + 1) * PIECE // STRIPE]
+                normed_piece = work.tile([P, PIECE], F32, name=f"normed{b}_{k}")
+                nc.vector.tensor_scalar(
+                    normed_piece[:], values[b][:].indirect(listed), SHIFT, SCALE, ALU.subtract, ALU.mult
+                )
+                normed.append(normed_piece)
+            for k in range(pieces):
+                listed = offsets[:, k * PIECE // STRIPE : (k + 1) * PIECE // STRIPE]
+                opened = work.tile([P, PIECE], F32, name=f"opened{b}_{k}")
+                nc.scalar.activation(opened[:], gates[b][:].indirect(listed), SIGMOID)
+                product = work.tile([P, PIECE], F32, name=f"product{b}_{k}")
+                nc.vector.tensor_tensor(product[:], normed[k][:], opened[:], ALU.mult)
+                nc.sync.dma_start(out[block_rows, k * PIECE : (k + 1) * PIECE], product[:])

@@ -25,6 +25,11 @@ def tile_lookup_gnorm_out_kernel(tc, tab, offs, out):
         tc.tile_pool(name="held", bufs=1) as held,
         tc.tile_pool(name="work", bufs=1) as work,
     ):
+        zero = held.tile([P, 1], F32, name="zero")
+        nc.vector.memset(zero[:], 0.0)
+        warm = held.tile([P, 1], F32, name="warm")
+        nc.scalar.activation(warm[:], zero[:], SIGMOID)
+
         offsets = held.tile([P, entries // STRIPE], U16, name="offsets")
         nc.sync.dma_start(offsets[:], offs)
 

@@ -15,9 +15,8 @@ SCALE = 1.5
 
 def tile_lookup_gnorm_out_kernel(tc, tab, offs, out):
     nc = tc.nc
-    tables, rows, places = tab.shape
-    assert tables == 2
-    entries = out.shape[1]
+    places = tab.shape[2]
+    rows, entries = out.shape
     blocks = rows // P
     pieces = entries // PIECE
 
@@ -33,31 +32,34 @@ def tile_lookup_gnorm_out_kernel(tc, tab, offs, out):
         offsets = held.tile([P, entries // STRIPE], U16, name="offsets")
         nc.sync.dma_start(offsets[:], offs)
 
-        values = []
-        gates = []
+        value_windows = []
+        gate_windows = []
         for b in range(blocks):
             block_rows = slice(b * P, (b + 1) * P)
             value_window = held.tile([P, places], F32, name=f"value_window{b}")
             nc.sync.dma_start(value_window[:], tab[0, block_rows, :])
             gate_window = held.tile([P, places], F32, name=f"gate_window{b}")
             nc.sync.dma_start(gate_window[:], tab[1, block_rows, :])
-            values.append(value_window)
-            gates.append(gate_window)
+            value_windows.append(value_window)
+            gate_windows.append(gate_window)
+
+        def look_up(b, k):
+            listed = offsets[:, k * PIECE // STRIPE : (k + 1) * PIECE // STRIPE]
+            normed = work.tile([P, PIECE], F32, name=f"normed{b}_{k}")
+            nc.vector.tensor_scalar(
+                normed[:], value_windows[b][:].indirect(listed), SHIFT, SCALE, ALU.subtract, ALU.mult
+            )
+            opened = work.tile([P, PIECE], F32, name=f"opened{b}_{k}")
+            nc.scalar.activation(opened[:], gate_windows[b][:].indirect(listed), SIGMOID)
+            return normed, opened
+
+        def finish(b, k, normed, opened):
+            product = work.tile([P, PIECE], F32, name=f"product{b}_{k}")
+            engine = nc.vector if b == blocks - 1 else nc.gpsimd
+            engine.tensor_tensor(product[:], normed[:], opened[:], ALU.mult)
+            nc.sync.dma_start(out[b * P : (b + 1) * P, k * PIECE : (k + 1) * PIECE], product[:])
 
         for b in range(blocks):
-            block_rows = slice(b * P, (b + 1) * P)
-            normed = []
+            halves = [look_up(b, k) for k in range(pieces)]
             for k in range(pieces):
-                listed = offsets[:, k * PIECE // STRIPE : (k + 1) * PIECE // STRIPE]
-                normed_piece = work.tile([P, PIECE], F32, name=f"normed{b}_{k}")
-                nc.vector.tensor_scalar(
-                    normed_piece[:], values[b][:].indirect(listed), SHIFT, SCALE, ALU.subtract, ALU.mult
-                )
-                normed.append(normed_piece)
-            for k in range(pieces):
-                listed = offsets[:, k * PIECE // STRIPE : (k + 1) * PIECE // STRIPE]
-                opened = work.tile([P, PIECE], F32, name=f"opened{b}_{k}")
-                nc.scalar.activation(opened[:], gates[b][:].indirect(listed), SIGMOID)
-                product = work.tile([P, PIECE], F32, name=f"product{b}_{k}")
-                nc.vector.tensor_tensor(product[:], normed[k][:], opened[:], ALU.mult)
-                nc.sync.dma_start(out[block_rows, k * PIECE : (k + 1) * PIECE], product[:])
+                finish(b, k, *halves[k])

@@ -7,7 +7,7 @@ SIGMOID = mybir.ActivationFunctionType.Sigmoid
 
 P = 128
 STRIPE = 16
-PIECE = 512
+SHORTEST = 96
 
 SHIFT = 0.125
 SCALE = 1.5
@@ -18,7 +18,12 @@ def tile_lookup_gnorm_out_kernel(tc, tab, offs, out):
     places = tab.shape[2]
     rows, entries = out.shape
     blocks = rows // P
-    pieces = entries // PIECE
+
+    cuts = [0]
+    while entries - cuts[-1] > SHORTEST:
+        cuts.append(cuts[-1] + max((entries - cuts[-1]) // 2, SHORTEST))
+    cuts.append(entries)
+    pieces = [slice(a, z) for a, z in zip(cuts, cuts[1:])]
 
     with (
         tc.tile_pool(name="held", bufs=1) as held,
@@ -43,23 +48,25 @@ def tile_lookup_gnorm_out_kernel(tc, tab, offs, out):
             value_windows.append(value_window)
             gate_windows.append(gate_window)
 
-        def look_up(b, k):
-            listed = offsets[:, k * PIECE // STRIPE : (k + 1) * PIECE // STRIPE]
-            normed = work.tile([P, PIECE], F32, name=f"normed{b}_{k}")
+        def look_up(b, piece):
+            length = piece.stop - piece.start
+            listed = offsets[:, piece.start // STRIPE : piece.stop // STRIPE]
+            normed = work.tile([P, length], F32, name=f"normed{b}_{piece.start}")
             nc.vector.tensor_scalar(
                 normed[:], value_windows[b][:].indirect(listed), SHIFT, SCALE, ALU.subtract, ALU.mult
             )
-            opened = work.tile([P, PIECE], F32, name=f"opened{b}_{k}")
+            opened = work.tile([P, length], F32, name=f"opened{b}_{piece.start}")
             nc.scalar.activation(opened[:], gate_windows[b][:].indirect(listed), SIGMOID)
             return normed, opened
 
-        def finish(b, k, normed, opened):
-            product = work.tile([P, PIECE], F32, name=f"product{b}_{k}")
+        def finish(b, piece, normed, opened):
+            length = piece.stop - piece.start
+            product = work.tile([P, length], F32, name=f"product{b}_{piece.start}")
             engine = nc.vector if b == blocks - 1 else nc.gpsimd
             engine.tensor_tensor(product[:], normed[:], opened[:], ALU.mult)
-            nc.sync.dma_start(out[b * P : (b + 1) * P, k * PIECE : (k + 1) * PIECE], product[:])
+            nc.sync.dma_start(out[b * P : (b + 1) * P, piece], product[:])
 
         for b in range(blocks):
-            halves = [look_up(b, k) for k in range(pieces)]
-            for k in range(pieces):
-                finish(b, k, *halves[k])
+            halves = [look_up(b, piece) for piece in pieces]
+            for piece, (normed, opened) in zip(pieces, halves):
+                finish(b, piece, normed, opened)

import concourse.mybir as mybir

F32 = mybir.dt.float32
U16 = mybir.dt.uint16
ALU = mybir.AluOpType
SIGMOID = mybir.ActivationFunctionType.Sigmoid

P = 128
STRIPE = 16
SHORTEST = 96

SHIFT = 0.125
SCALE = 1.5


def tile_lookup_gnorm_out_kernel(tc, tab, offs, out):
    nc = tc.nc
    places = tab.shape[2]
    rows, entries = out.shape
    blocks = rows // P

    cuts = [0]
    while entries - cuts[-1] > SHORTEST:
        cuts.append(cuts[-1] + max((entries - cuts[-1]) // 2, SHORTEST))
    cuts.append(entries)
    pieces = [slice(a, z) for a, z in zip(cuts, cuts[1:])]

    with (
        tc.tile_pool(name="held", bufs=1) as held,
        tc.tile_pool(name="work", bufs=1) as work,
    ):
        zero = held.tile([P, 1], F32, name="zero")
        nc.vector.memset(zero[:], 0.0)
        warm = held.tile([P, 1], F32, name="warm")
        nc.scalar.activation(warm[:], zero[:], SIGMOID)

        offsets = held.tile([P, entries // STRIPE], U16, name="offsets")
        nc.sync.dma_start(offsets[:], offs)

        value_windows = []
        gate_windows = []
        for b in range(blocks):
            block_rows = slice(b * P, (b + 1) * P)
            value_window = held.tile([P, places], F32, name=f"value_window{b}")
            nc.sync.dma_start(value_window[:], tab[0, block_rows, :])
            gate_window = held.tile([P, places], F32, name=f"gate_window{b}")
            nc.sync.dma_start(gate_window[:], tab[1, block_rows, :])
            value_windows.append(value_window)
            gate_windows.append(gate_window)

        def look_up(b, piece):
            length = piece.stop - piece.start
            listed = offsets[:, piece.start // STRIPE : piece.stop // STRIPE]
            normed = work.tile([P, length], F32, name=f"normed{b}_{piece.start}")
            nc.vector.tensor_scalar(
                normed[:], value_windows[b][:].indirect(listed), SHIFT, SCALE, ALU.subtract, ALU.mult
            )
            opened = work.tile([P, length], F32, name=f"opened{b}_{piece.start}")
            nc.scalar.activation(opened[:], gate_windows[b][:].indirect(listed), SIGMOID)
            return normed, opened

        def finish(b, piece, normed, opened):
            length = piece.stop - piece.start
            product = work.tile([P, length], F32, name=f"product{b}_{piece.start}")
            engine = nc.vector if b == blocks - 1 else nc.gpsimd
            engine.tensor_tensor(product[:], normed[:], opened[:], ALU.mult)
            nc.sync.dma_start(out[b * P : (b + 1) * P, piece], product[:])

        for b in range(blocks):
            halves = [look_up(b, piece) for piece in pieces]
            for piece, (normed, opened) in zip(pieces, halves):
                finish(b, piece, normed, opened)
